import numpy as np
import ml_dtypes

BF16 = ml_dtypes.bfloat16


def bf(x):
    return np.asarray(x, np.float32).astype(BF16)


def f32(x):
    return np.asarray(x, np.float32)


def f64(x):
    return np.asarray(x).astype(np.float64)


def striped(idx):
    return np.tile(idx.reshape(-1, 16).T, (8, 1))


S, K, M, N, D, V = 1024, 128, 256, 512, 4, 128


def setup_inputs():
    return {"table": bf(np.random.standard_normal((K, S))), "w": bf(np.random.standard_normal((K, M)) / np.sqrt(D * K)), "b": f32(0.5 * np.random.standard_normal((M, 1))), "offs": striped(np.random.permutation(np.tile(np.arange(S), 2))[:N])}


def reference(table, w, b, offs):
    idx = offs[:16].T.reshape(-1)
    x = f64(table)[:, idx]
    y = f64(w).T @ sum(x[:, t * V : (t + 1) * V] for t in range(D))
    return np.tanh(y + f64(b))

@@ -1,0 +1,47 @@
+import concourse.mybir as mybir
+
+BF16, F32, U16 = mybir.dt.bfloat16, mybir.dt.float32, mybir.dt.uint16
+TANH = mybir.ActivationFunctionType.Tanh
+
+P = 128
+NODES = 1024
+OUT_FEATURES = 256
+OUT_NODES = 128
+NEIGHBOURS = 4
+LIST = NEIGHBOURS * OUT_NODES
+PIECE_COLUMNS = OUT_NODES // 16
+BLOCKS = OUT_FEATURES // P
+
+FLOPS = 2 * P * OUT_FEATURES * LIST
+
+
+def tile_gather_matmul_kernel(tc, table, w, b, offs, out):
+    nc = tc.nc
+    with (
+        tc.tile_pool(name="held", bufs=1) as held,
+        tc.psum_pool(name="psum", bufs=1) as psum,
+    ):
+        offsets = held.tile([P, LIST // 16], U16, name="offsets")
+        nc.sync.dma_start(offsets[:], offs)
+        nodes = held.tile([P, NODES], BF16, name="nodes")
+        nc.sync.dma_start(nodes[:], table)
+        weights = held.tile([P, OUT_FEATURES], BF16, name="weights")
+        nc.scalar.dma_start(weights[:], w)
+        bias = held.tile([P, BLOCKS], F32, name="bias")
+        with nc.allow_non_contiguous_dma(reason="256 bias values, one to a partition and block"):
+            nc.scalar.dma_start(bias[:], b.rearrange("(a p) o -> p (a o)", p=P))
+
+        for a in range(BLOCKS):
+            bank = psum.tile([P, OUT_NODES], F32, name=f"bank{a}")
+            for t in range(NEIGHBOURS):
+                piece = offsets[:, t * PIECE_COLUMNS : (t + 1) * PIECE_COLUMNS]
+                nc.tensor.matmul(
+                    bank[:],
+                    weights[:, a * P : (a + 1) * P],
+                    nodes[:].indirect(piece),
+                    start=(t == 0),
+                    stop=(t == NEIGHBOURS - 1),
+                )
+            result = held.tile([P, OUT_NODES], F32, name=f"result{a}")
+            nc.scalar.activation(result[:], bank[:], TANH, bias=bias[:, a : a + 1])
+            nc.sync.dma_start(out[a * P : (a + 1) * P, :], result[:])

@@ -24,12 +24,17 @@ def tile_gather_matmul_kernel(tc, table, w, b, offs, out):
         offsets = held.tile([P, LIST // 16], U16, name="offsets")
         nc.sync.dma_start(offsets[:], offs)
         nodes = held.tile([P, NODES], BF16, name="nodes")
-        nc.sync.dma_start(nodes[:], table)
+        nc.scalar.dma_start(nodes[:], table)
         weights = held.tile([P, OUT_FEATURES], BF16, name="weights")
-        nc.scalar.dma_start(weights[:], w)
+        nc.sync.dma_start(weights[:], w)
         bias = held.tile([P, BLOCKS], F32, name="bias")
         with nc.allow_non_contiguous_dma(reason="256 bias values, one to a partition and block"):
-            nc.scalar.dma_start(bias[:], b.rearrange("(a p) o -> p (a o)", p=P))
+            nc.sync.dma_start(bias[:], b.rearrange("(a p) o -> p (a o)", p=P))
+
+        zero = held.tile([P, 1], F32, name="zero")
+        nc.vector.memset(zero[:], 0.0)
+        warm = held.tile([P, 1], F32, name="warm")
+        nc.scalar.activation(warm[:], zero[:], TANH)
 
         for a in range(BLOCKS):
             bank = psum.tile([P, OUT_NODES], F32, name=f"bank{a}")

@@ -11,6 +11,7 @@ NEIGHBOURS = 4
 LIST = NEIGHBOURS * OUT_NODES
 PIECE_COLUMNS = OUT_NODES // 16
 BLOCKS = OUT_FEATURES // P
+WARM_MATMULS = 16
 
 FLOPS = 2 * P * OUT_FEATURES * LIST
 
@@ -31,10 +32,13 @@ def tile_gather_matmul_kernel(tc, table, w, b, offs, out):
         with nc.allow_non_contiguous_dma(reason="256 bias values, one to a partition and block"):
             nc.sync.dma_start(bias[:], b.rearrange("(a p) o -> p (a o)", p=P))
 
-        zero = held.tile([P, 1], F32, name="zero")
-        nc.vector.memset(zero[:], 0.0)
-        warm = held.tile([P, 1], F32, name="warm")
-        nc.scalar.activation(warm[:], zero[:], TANH)
+        zeros = held.tile([P, P], BF16, name="zeros")
+        nc.vector.memset(zeros[:], 0.0)
+        idle_bank = psum.tile([P, P], F32, name="idle_bank")
+        for i in range(WARM_MATMULS):
+            nc.tensor.matmul(idle_bank[:], zeros[:], zeros[:], start=True, stop=True)
+        idle_tanh = held.tile([P, 1], F32, name="idle_tanh")
+        nc.scalar.activation(idle_tanh[:], zeros[:, 0:1], TANH)
 
         for a in range(BLOCKS):
             bank = psum.tile([P, OUT_NODES], F32, name=f"bank{a}")

@@ -30,7 +30,7 @@ def tile_gather_matmul_kernel(tc, table, w, b, offs, out):
         nc.sync.dma_start(weights[:], w)
         bias = held.tile([P, BLOCKS], F32, name="bias")
         with nc.allow_non_contiguous_dma(reason="256 bias values, one to a partition and block"):
-            nc.sync.dma_start(bias[:], b.rearrange("(a p) o -> p (a o)", p=P))
+            nc.scalar.dma_start(bias[:], b.rearrange("(a p) o -> p (a o)", p=P))
 
         zeros = held.tile([P, P], BF16, name="zeros")
         nc.vector.memset(zeros[:], 0.0)

@@ -11,7 +11,6 @@ NEIGHBOURS = 4
 LIST = NEIGHBOURS * OUT_NODES
 PIECE_COLUMNS = OUT_NODES // 16
 BLOCKS = OUT_FEATURES // P
-WARM_MATMULS = 16
 
 FLOPS = 2 * P * OUT_FEATURES * LIST
 
@@ -32,13 +31,10 @@ def tile_gather_matmul_kernel(tc, table, w, b, offs, out):
         with nc.allow_non_contiguous_dma(reason="256 bias values, one to a partition and block"):
             nc.scalar.dma_start(bias[:], b.rearrange("(a p) o -> p (a o)", p=P))
 
-        zeros = held.tile([P, P], BF16, name="zeros")
+        zeros = held.tile([P, 1], F32, name="zeros")
         nc.vector.memset(zeros[:], 0.0)
-        idle_bank = psum.tile([P, P], F32, name="idle_bank")
-        for i in range(WARM_MATMULS):
-            nc.tensor.matmul(idle_bank[:], zeros[:], zeros[:], start=True, stop=True)
         idle_tanh = held.tile([P, 1], F32, name="idle_tanh")
-        nc.scalar.activation(idle_tanh[:], zeros[:, 0:1], TANH)
+        nc.scalar.activation(idle_tanh[:], zeros[:], TANH)
 
         for a in range(BLOCKS):
             bank = psum.tile([P, OUT_NODES], F32, name=f"bank{a}")

@@ -11,6 +11,7 @@ NEIGHBOURS = 4
 LIST = NEIGHBOURS * OUT_NODES
 PIECE_COLUMNS = OUT_NODES // 16
 BLOCKS = OUT_FEATURES // P
+BURST = 256
 
 FLOPS = 2 * P * OUT_FEATURES * LIST
 
@@ -23,9 +24,9 @@ def tile_gather_matmul_kernel(tc, table, w, b, offs, out):
     ):
         offsets = held.tile([P, LIST // 16], U16, name="offsets")
         nc.sync.dma_start(offsets[:], offs)
-        nodes = held.tile([P, NODES], BF16, name="nodes")
+        nodes = held.tile([P, NODES], BF16, name="nodes", align_bytes=BURST)
         nc.scalar.dma_start(nodes[:], table)
-        weights = held.tile([P, OUT_FEATURES], BF16, name="weights")
+        weights = held.tile([P, OUT_FEATURES], BF16, name="weights", align_bytes=BURST)
         nc.sync.dma_start(weights[:], w)
         bias = held.tile([P, BLOCKS], F32, name="bias")
         with nc.allow_non_contiguous_dma(reason="256 bias values, one to a partition and block"):
@@ -47,6 +48,6 @@ def tile_gather_matmul_kernel(tc, table, w, b, offs, out):
                     start=(t == 0),
                     stop=(t == NEIGHBOURS - 1),
                 )
-            result = held.tile([P, OUT_NODES], F32, name=f"result{a}")
+            result = held.tile([P, OUT_NODES], F32, name=f"result{a}", align_bytes=BURST)
             nc.scalar.activation(result[:], bank[:], TANH, bias=bias[:, a : a + 1])
             nc.sync.dma_start(out[a * P : (a + 1) * P, :], result[:])

@@ -22,12 +22,12 @@ def tile_gather_matmul_kernel(tc, table, w, b, offs, out):
         tc.tile_pool(name="held", bufs=1) as held,
         tc.psum_pool(name="psum", bufs=1) as psum,
     ):
-        offsets = held.tile([P, LIST // 16], U16, name="offsets")
-        nc.sync.dma_start(offsets[:], offs)
-        nodes = held.tile([P, NODES], BF16, name="nodes", align_bytes=BURST)
-        nc.scalar.dma_start(nodes[:], table)
         weights = held.tile([P, OUT_FEATURES], BF16, name="weights", align_bytes=BURST)
         nc.sync.dma_start(weights[:], w)
+        nodes = held.tile([P, NODES], BF16, name="nodes", align_bytes=BURST)
+        nc.scalar.dma_start(nodes[:], table)
+        offsets = held.tile([P, LIST // 16], U16, name="offsets")
+        nc.sync.dma_start(offsets[:], offs)
         bias = held.tile([P, BLOCKS], F32, name="bias")
         with nc.allow_non_contiguous_dma(reason="256 bias values, one to a partition and block"):
             nc.scalar.dma_start(bias[:], b.rearrange("(a p) o -> p (a o)", p=P))

@@ -22,12 +22,16 @@ def tile_gather_matmul_kernel(tc, table, w, b, offs, out):
         tc.tile_pool(name="held", bufs=1) as held,
         tc.psum_pool(name="psum", bufs=1) as psum,
     ):
-        weights = held.tile([P, OUT_FEATURES], BF16, name="weights", align_bytes=BURST)
-        nc.sync.dma_start(weights[:], w)
+        weights = [
+            held.tile([P, P], BF16, name=f"weights{a}", align_bytes=BURST) for a in range(BLOCKS)
+        ]
+        nc.sync.dma_start(weights[0][:], w[:, 0:P])
         nodes = held.tile([P, NODES], BF16, name="nodes", align_bytes=BURST)
         nc.scalar.dma_start(nodes[:], table)
         offsets = held.tile([P, LIST // 16], U16, name="offsets")
         nc.sync.dma_start(offsets[:], offs)
+        for a in range(1, BLOCKS):
+            nc.scalar.dma_start(weights[a][:], w[:, a * P : (a + 1) * P])
         bias = held.tile([P, BLOCKS], F32, name="bias")
         with nc.allow_non_contiguous_dma(reason="256 bias values, one to a partition and block"):
             nc.scalar.dma_start(bias[:], b.rearrange("(a p) o -> p (a o)", p=P))
@@ -43,7 +47,7 @@ def tile_gather_matmul_kernel(tc, table, w, b, offs, out):
                 piece = offsets[:, t * PIECE_COLUMNS : (t + 1) * PIECE_COLUMNS]
                 nc.tensor.matmul(
                     bank[:],
-                    weights[:, a * P : (a + 1) * P],
+                    weights[a][:],
                     nodes[:].indirect(piece),
                     start=(t == 0),
                     stop=(t == NEIGHBOURS - 1),

@@ -28,6 +28,8 @@ def tile_gather_matmul_kernel(tc, table, w, b, offs, out):
         nc.sync.dma_start(weights[0][:], w[:, 0:P])
         nodes = held.tile([P, NODES], BF16, name="nodes", align_bytes=BURST)
         nc.scalar.dma_start(nodes[:], table)
+        spare = held.tile([16, 16], BF16, name="spare")
+        nc.scalar.dma_start(spare[:], w[0:16, P : P + 16])
         offsets = held.tile([P, LIST // 16], U16, name="offsets")
         nc.sync.dma_start(offsets[:], offs)
         for a in range(1, BLOCKS):

import concourse.mybir as mybir

BF16, F32, U16 = mybir.dt.bfloat16, mybir.dt.float32, mybir.dt.uint16
TANH = mybir.ActivationFunctionType.Tanh

P = 128
NODES = 1024
OUT_FEATURES = 256
OUT_NODES = 128
NEIGHBOURS = 4
LIST = NEIGHBOURS * OUT_NODES
PIECE_COLUMNS = OUT_NODES // 16
BLOCKS = OUT_FEATURES // P
BURST = 256

FLOPS = 2 * P * OUT_FEATURES * LIST


def tile_gather_matmul_kernel(tc, table, w, b, offs, out):
    nc = tc.nc
    with (
        tc.tile_pool(name="held", bufs=1) as held,
        tc.psum_pool(name="psum", bufs=1) as psum,
    ):
        weights = [
            held.tile([P, P], BF16, name=f"weights{a}", align_bytes=BURST) for a in range(BLOCKS)
        ]
        nc.sync.dma_start(weights[0][:], w[:, 0:P])
        nodes = held.tile([P, NODES], BF16, name="nodes", align_bytes=BURST)
        nc.scalar.dma_start(nodes[:], table)
        spare = held.tile([16, 16], BF16, name="spare")
        nc.scalar.dma_start(spare[:], w[0:16, P : P + 16])
        offsets = held.tile([P, LIST // 16], U16, name="offsets")
        nc.sync.dma_start(offsets[:], offs)
        for a in range(1, BLOCKS):
            nc.scalar.dma_start(weights[a][:], w[:, a * P : (a + 1) * P])
        bias = held.tile([P, BLOCKS], F32, name="bias")
        with nc.allow_non_contiguous_dma(reason="256 bias values, one to a partition and block"):
            nc.scalar.dma_start(bias[:], b.rearrange("(a p) o -> p (a o)", p=P))

        zeros = held.tile([P, 1], F32, name="zeros")
        nc.vector.memset(zeros[:], 0.0)
        idle_tanh = held.tile([P, 1], F32, name="idle_tanh")
        nc.scalar.activation(idle_tanh[:], zeros[:], TANH)

        for a in range(BLOCKS):
            bank = psum.tile([P, OUT_NODES], F32, name=f"bank{a}")
            for t in range(NEIGHBOURS):
                piece = offsets[:, t * PIECE_COLUMNS : (t + 1) * PIECE_COLUMNS]
                nc.tensor.matmul(
                    bank[:],
                    weights[a][:],
                    nodes[:].indirect(piece),
                    start=(t == 0),
                    stop=(t == NEIGHBOURS - 1),
                )
            result = held.tile([P, OUT_NODES], F32, name=f"result{a}", align_bytes=BURST)
            nc.scalar.activation(result[:], bank[:], TANH, bias=bias[:, a : a + 1])
            nc.sync.dma_start(out[a * P : (a + 1) * P, :], result[:])
